import numpy as np
import ml_dtypes

BF16 = ml_dtypes.bfloat16


def bf(x):
    return np.asarray(x, np.float32).astype(BF16)


def f32(x):
    return np.asarray(x, np.float32)


def f64(x):
    return np.asarray(x).astype(np.float64)


def striped(idx):
    return np.tile(idx.reshape(-1, 16).T, (8, 1))


S, K, M, N = 1024, 128, 256, 1024


def setup_inputs():
    return {"table": bf(np.random.standard_normal((S, K))), "w": bf(np.random.standard_normal((K, M)) / np.sqrt(K)), "b": f32(0.5 * np.random.standard_normal((M, 1))), "offs": striped(np.random.permutation(S))}


def reference(table, w, b, offs):
    idx = offs[:16].T.reshape(-1)
    x = f64(table)[idx].T
    y = f64(w).T @ x
    return np.maximum(y + f64(b), 0.0)

@@ -1,0 +1,60 @@
+import concourse.mybir as mybir
+from concourse.masks import make_identity
+
+P = 128
+S, K, M, N = 1024, 128, 256, 1024
+PIECE = 512
+FLOPS = 2 * K * M * N
+
+BF16, F32, U16 = mybir.dt.bfloat16, mybir.dt.float32, mybir.dt.uint16
+RELU = mybir.ActivationFunctionType.Relu
+ADD, MAX = mybir.AluOpType.add, mybir.AluOpType.max
+
+
+def tile_gather_matmul_kernel(tc, table, w, b, offs, out):
+    nc = tc.nc
+    blocks = S // P
+    half = blocks // 2
+    with (
+        tc.tile_pool(name="held", bufs=1) as held,
+        tc.tile_pool(name="results", bufs=4) as results,
+        tc.psum_pool(name="flips", bufs=1) as flips,
+        tc.psum_pool(name="banks", bufs=4) as banks,
+    ):
+        offsets = held.tile([P, N // 16], U16, name="offsets")
+        nc.sync.dma_start(offsets[:], offs)
+
+        tokens = held.tile([P, blocks, K], BF16, name="tokens")
+        by_block = table.rearrange("(a p) k -> p a k", p=P)
+        nc.sync.dma_start(tokens[:, 0:half, :], by_block[:, 0:half, :])
+        nc.scalar.dma_start(tokens[:, half:blocks, :], by_block[:, half:blocks, :])
+
+        weights = held.tile([K, M], BF16, name="weights")
+        nc.scalar.dma_start(weights[:], w)
+
+        identity = held.tile([P, P], BF16, name="identity")
+        make_identity(nc, identity[:])
+
+        bias = held.tile([P, M // P], F32, name="bias")
+        nc.gpsimd.dma_start(bias[:], b.rearrange("(a p) o -> p (a o)", p=P))
+
+        window = held.tile([K, S], BF16, name="window")
+        flipped = [flips.tile([K, half * P], BF16, name="flipped%d" % h) for h in range(2)]
+        for a in range(blocks):
+            h, j = divmod(a, half)
+            nc.tensor.transpose(flipped[h][:, j * P : (j + 1) * P], tokens[:, a, :], identity[:])
+        nc.vector.tensor_copy(window[:, 0 : half * P], flipped[0][:])
+        nc.scalar.copy(window[:, half * P : S], flipped[1][:])
+
+        for piece in range(N // PIECE):
+            picked = window[:].indirect(offsets[:, piece * (PIECE // 16) : (piece + 1) * (PIECE // 16)])
+            for a in range(M // P):
+                bank = banks.tile([P, PIECE], F32, name="bank")
+                nc.tensor.matmul(bank[:], weights[:, a * P : (a + 1) * P], picked, start=True, stop=True)
+                result = results.tile([P, PIECE], F32, name="result")
+                if a == 0:
+                    nc.scalar.activation(result[:], bank[:], RELU, bias=bias[:, a : a + 1])
+                    nc.scalar.dma_start(out[a * P : (a + 1) * P, piece * PIECE : (piece + 1) * PIECE], result[:])
+                else:
+                    nc.vector.tensor_scalar(result[:], bank[:], bias[:, a : a + 1], 0.0, ADD, MAX)
+                    nc.sync.dma_start(out[a * P : (a + 1) * P, piece * PIECE : (piece + 1) * PIECE], result[:])

@@ -13,38 +13,40 @@ ADD, MAX = mybir.AluOpType.add, mybir.AluOpType.max
 
 def tile_gather_matmul_kernel(tc, table, w, b, offs, out):
     nc = tc.nc
-    blocks = S // P
-    half = blocks // 2
+    pairs = S // (2 * P)
     with (
         tc.tile_pool(name="held", bufs=1) as held,
         tc.tile_pool(name="results", bufs=4) as results,
-        tc.psum_pool(name="flips", bufs=1) as flips,
+        tc.psum_pool(name="flips", bufs=4) as flips,
         tc.psum_pool(name="banks", bufs=4) as banks,
     ):
+        tokens = held.tile([P, 2 * pairs, K], BF16, name="tokens")
+        by_block = table.rearrange("(a p) k -> p a k", p=P)
+        for q in range(pairs):
+            queue = nc.sync if q % 2 == 0 else nc.scalar
+            queue.dma_start(tokens[:, 2 * q : 2 * q + 2, :], by_block[:, 2 * q : 2 * q + 2, :])
+
         offsets = held.tile([P, N // 16], U16, name="offsets")
         nc.sync.dma_start(offsets[:], offs)
-
-        tokens = held.tile([P, blocks, K], BF16, name="tokens")
-        by_block = table.rearrange("(a p) k -> p a k", p=P)
-        nc.sync.dma_start(tokens[:, 0:half, :], by_block[:, 0:half, :])
-        nc.scalar.dma_start(tokens[:, half:blocks, :], by_block[:, half:blocks, :])
 
         weights = held.tile([K, M], BF16, name="weights")
         nc.scalar.dma_start(weights[:], w)
 
+        bias = held.tile([P, M // P], F32, name="bias")
+        nc.sync.dma_start(bias[:], b.rearrange("(a p) o -> p (a o)", p=P))
+
         identity = held.tile([P, P], BF16, name="identity")
         make_identity(nc, identity[:])
 
-        bias = held.tile([P, M // P], F32, name="bias")
-        nc.gpsimd.dma_start(bias[:], b.rearrange("(a p) o -> p (a o)", p=P))
-
         window = held.tile([K, S], BF16, name="window")
-        flipped = [flips.tile([K, half * P], BF16, name="flipped%d" % h) for h in range(2)]
-        for a in range(blocks):
-            h, j = divmod(a, half)
-            nc.tensor.transpose(flipped[h][:, j * P : (j + 1) * P], tokens[:, a, :], identity[:])
-        nc.vector.tensor_copy(window[:, 0 : half * P], flipped[0][:])
-        nc.scalar.copy(window[:, half * P : S], flipped[1][:])
+        for q in range(pairs):
+            flipped = flips.tile([K, 2 * P], BF16, name="flipped")
+            for j in range(2):
+                nc.tensor.transpose(flipped[:, j * P : (j + 1) * P], tokens[:, 2 * q + j, :], identity[:])
+            if q % 2 == 0:
+                nc.scalar.copy(window[:, 2 * q * P : (2 * q + 2) * P], flipped[:])
+            else:
+                nc.vector.tensor_copy(window[:, 2 * q * P : (2 * q + 2) * P], flipped[:])
 
         for piece in range(N // PIECE):
             picked = window[:].indirect(offsets[:, piece * (PIECE // 16) : (piece + 1) * (PIECE // 16)])

@@ -4,6 +4,7 @@ from concourse.masks import make_identity
 P = 128
 S, K, M, N = 1024, 128, 256, 1024
 PIECE = 512
+WARMING = 5
 FLOPS = 2 * K * M * N
 
 BF16, F32, U16 = mybir.dt.bfloat16, mybir.dt.float32, mybir.dt.uint16
@@ -20,6 +21,12 @@ def tile_gather_matmul_kernel(tc, table, w, b, offs, out):
         tc.psum_pool(name="flips", bufs=4) as flips,
         tc.psum_pool(name="banks", bufs=4) as banks,
     ):
+        zeros = held.tile([P, PIECE], BF16, name="zeros")
+        nc.vector.memset(zeros[:], 0.0)
+        unread = banks.tile([P, PIECE], F32, tag="bank")
+        for i in range(WARMING):
+            nc.tensor.matmul(unread[:], zeros[:, 0:P], zeros[:], start=True, stop=True)
+
         tokens = held.tile([P, 2 * pairs, K], BF16, name="tokens")
         by_block = table.rearrange("(a p) k -> p a k", p=P)
         for q in range(pairs):

@@ -3,8 +3,7 @@ from concourse.masks import make_identity
 
 P = 128
 S, K, M, N = 1024, 128, 256, 1024
-PIECE = 512
-WARMING = 5
+PIECE = 256
 FLOPS = 2 * K * M * N
 
 BF16, F32, U16 = mybir.dt.bfloat16, mybir.dt.float32, mybir.dt.uint16
@@ -17,16 +16,10 @@ def tile_gather_matmul_kernel(tc, table, w, b, offs, out):
     pairs = S // (2 * P)
     with (
         tc.tile_pool(name="held", bufs=1) as held,
-        tc.tile_pool(name="results", bufs=4) as results,
+        tc.tile_pool(name="results", bufs=(N // PIECE) * (M // P)) as results,
         tc.psum_pool(name="flips", bufs=4) as flips,
         tc.psum_pool(name="banks", bufs=4) as banks,
     ):
-        zeros = held.tile([P, PIECE], BF16, name="zeros")
-        nc.vector.memset(zeros[:], 0.0)
-        unread = banks.tile([P, PIECE], F32, tag="bank")
-        for i in range(WARMING):
-            nc.tensor.matmul(unread[:], zeros[:, 0:P], zeros[:], start=True, stop=True)
-
         tokens = held.tile([P, 2 * pairs, K], BF16, name="tokens")
         by_block = table.rearrange("(a p) k -> p a k", p=P)
         for q in range(pairs):

@@ -23,14 +23,13 @@ def tile_gather_matmul_kernel(tc, table, w, b, offs, out):
         tokens = held.tile([P, 2 * pairs, K], BF16, name="tokens")
         by_block = table.rearrange("(a p) k -> p a k", p=P)
         for q in range(pairs):
-            queue = nc.sync if q % 2 == 0 else nc.scalar
-            queue.dma_start(tokens[:, 2 * q : 2 * q + 2, :], by_block[:, 2 * q : 2 * q + 2, :])
+            nc.sync.dma_start(tokens[:, 2 * q : 2 * q + 2, :], by_block[:, 2 * q : 2 * q + 2, :])
 
         offsets = held.tile([P, N // 16], U16, name="offsets")
         nc.sync.dma_start(offsets[:], offs)
 
         weights = held.tile([K, M], BF16, name="weights")
-        nc.scalar.dma_start(weights[:], w)
+        nc.sync.dma_start(weights[:], w)
 
         bias = held.tile([P, M // P], F32, name="bias")
         nc.sync.dma_start(bias[:], b.rearrange("(a p) o -> p (a o)", p=P))

@@ -55,7 +55,6 @@ def tile_gather_matmul_kernel(tc, table, w, b, offs, out):
                 result = results.tile([P, PIECE], F32, name="result")
                 if a == 0:
                     nc.scalar.activation(result[:], bank[:], RELU, bias=bias[:, a : a + 1])
-                    nc.scalar.dma_start(out[a * P : (a + 1) * P, piece * PIECE : (piece + 1) * PIECE], result[:])
                 else:
                     nc.vector.tensor_scalar(result[:], bank[:], bias[:, a : a + 1], 0.0, ADD, MAX)
-                    nc.sync.dma_start(out[a * P : (a + 1) * P, piece * PIECE : (piece + 1) * PIECE], result[:])
+                nc.sync.dma_start(out[a * P : (a + 1) * P, piece * PIECE : (piece + 1) * PIECE], result[:])

@@ -17,8 +17,7 @@ def tile_gather_matmul_kernel(tc, table, w, b, offs, out):
     with (
         tc.tile_pool(name="held", bufs=1) as held,
         tc.tile_pool(name="results", bufs=(N // PIECE) * (M // P)) as results,
-        tc.psum_pool(name="flips", bufs=4) as flips,
-        tc.psum_pool(name="banks", bufs=4) as banks,
+        tc.psum_pool(name="banks", bufs=8) as banks,
     ):
         tokens = held.tile([P, 2 * pairs, K], BF16, name="tokens")
         by_block = table.rearrange("(a p) k -> p a k", p=P)
@@ -38,14 +37,13 @@ def tile_gather_matmul_kernel(tc, table, w, b, offs, out):
         make_identity(nc, identity[:])
 
         window = held.tile([K, S], BF16, name="window")
-        for q in range(pairs):
-            flipped = flips.tile([K, 2 * P], BF16, name="flipped")
-            for j in range(2):
-                nc.tensor.transpose(flipped[:, j * P : (j + 1) * P], tokens[:, 2 * q + j, :], identity[:])
-            if q % 2 == 0:
-                nc.scalar.copy(window[:, 2 * q * P : (2 * q + 2) * P], flipped[:])
+        for t in range(S // P):
+            flipped = banks.tile([K, P], BF16, name="flipped", tag="bank")
+            nc.tensor.transpose(flipped[:], tokens[:, t, :], identity[:])
+            if t % 2 == 0:
+                nc.scalar.copy(window[:, t * P : (t + 1) * P], flipped[:])
             else:
-                nc.vector.tensor_copy(window[:, 2 * q * P : (2 * q + 2) * P], flipped[:])
+                nc.vector.tensor_copy(window[:, t * P : (t + 1) * P], flipped[:])
 
         for piece in range(N // PIECE):
             picked = window[:].indirect(offsets[:, piece * (PIECE // 16) : (piece + 1) * (PIECE // 16)])

@@ -13,16 +13,19 @@ ADD, MAX = mybir.AluOpType.add, mybir.AluOpType.max
 
 def tile_gather_matmul_kernel(tc, table, w, b, offs, out):
     nc = tc.nc
-    pairs = S // (2 * P)
     with (
         tc.tile_pool(name="held", bufs=1) as held,
         tc.tile_pool(name="results", bufs=(N // PIECE) * (M // P)) as results,
         tc.psum_pool(name="banks", bufs=8) as banks,
     ):
-        tokens = held.tile([P, 2 * pairs, K], BF16, name="tokens")
-        by_block = table.rearrange("(a p) k -> p a k", p=P)
-        for q in range(pairs):
-            nc.sync.dma_start(tokens[:, 2 * q : 2 * q + 2, :], by_block[:, 2 * q : 2 * q + 2, :])
+        tokens = held.tile([P, S // P, K], BF16, name="tokens")
+        by_block = table.rearrange("(t p) k -> p t k", p=P)
+        first_block = 0
+        for blocks in (1, 1, 2, 2, 2):
+            nc.sync.dma_start(
+                tokens[:, first_block : first_block + blocks, :], by_block[:, first_block : first_block + blocks, :]
+            )
+            first_block += blocks
 
         offsets = held.tile([P, N // 16], U16, name="offsets")
         nc.sync.dma_start(offsets[:], offs)

@@ -21,7 +21,7 @@ def tile_gather_matmul_kernel(tc, table, w, b, offs, out):
         tokens = held.tile([P, S // P, K], BF16, name="tokens")
         by_block = table.rearrange("(t p) k -> p t k", p=P)
         first_block = 0
-        for blocks in (1, 1, 2, 2, 2):
+        for blocks in (2, 2, 2, 1, 1):
             nc.sync.dma_start(
                 tokens[:, first_block : first_block + blocks, :], by_block[:, first_block : first_block + blocks, :]
             )

@@ -7,7 +7,6 @@ PIECE = 256
 FLOPS = 2 * K * M * N
 
 BF16, F32, U16 = mybir.dt.bfloat16, mybir.dt.float32, mybir.dt.uint16
-RELU = mybir.ActivationFunctionType.Relu
 ADD, MAX = mybir.AluOpType.add, mybir.AluOpType.max
 
 
@@ -43,10 +42,7 @@ def tile_gather_matmul_kernel(tc, table, w, b, offs, out):
         for t in range(S // P):
             flipped = banks.tile([K, P], BF16, name="flipped", tag="bank")
             nc.tensor.transpose(flipped[:], tokens[:, t, :], identity[:])
-            if t % 2 == 0:
-                nc.scalar.copy(window[:, t * P : (t + 1) * P], flipped[:])
-            else:
-                nc.vector.tensor_copy(window[:, t * P : (t + 1) * P], flipped[:])
+            nc.vector.tensor_copy(window[:, t * P : (t + 1) * P], flipped[:])
 
         for piece in range(N // PIECE):
             picked = window[:].indirect(offsets[:, piece * (PIECE // 16) : (piece + 1) * (PIECE // 16)])
@@ -54,8 +50,5 @@ def tile_gather_matmul_kernel(tc, table, w, b, offs, out):
                 bank = banks.tile([P, PIECE], F32, name="bank")
                 nc.tensor.matmul(bank[:], weights[:, a * P : (a + 1) * P], picked, start=True, stop=True)
                 result = results.tile([P, PIECE], F32, name="result")
-                if a == 0:
-                    nc.scalar.activation(result[:], bank[:], RELU, bias=bias[:, a : a + 1])
-                else:
-                    nc.vector.tensor_scalar(result[:], bank[:], bias[:, a : a + 1], 0.0, ADD, MAX)
+                nc.vector.tensor_scalar(result[:], bank[:], bias[:, a : a + 1], 0.0, ADD, MAX)
                 nc.sync.dma_start(out[a * P : (a + 1) * P, piece * PIECE : (piece + 1) * PIECE], result[:])

@@ -3,6 +3,7 @@ from concourse.masks import make_identity
 
 P = 128
 S, K, M, N = 1024, 128, 256, 1024
+BANK = 512
 PIECE = 256
 FLOPS = 2 * K * M * N
 
@@ -38,11 +39,24 @@ def tile_gather_matmul_kernel(tc, table, w, b, offs, out):
         identity = held.tile([P, P], BF16, name="identity")
         make_identity(nc, identity[:])
 
+        zeros = held.tile([P, P], BF16, name="zeros")
+        nc.vector.memset(zeros[:], 0.0)
+        for columns in (BANK, BANK, BANK // 2):
+            unread = banks.tile([P, columns // P, P], F32, name="unread", tag="bank")
+            nc.tensor.matmul(
+                unread[:], zeros[:], zeros[:].unsqueeze(1).to_broadcast([P, columns // P, P]), start=True, stop=True
+            )
+
         window = held.tile([K, S], BF16, name="window")
         for t in range(S // P):
             flipped = banks.tile([K, P], BF16, name="flipped", tag="bank")
             nc.tensor.transpose(flipped[:], tokens[:, t, :], identity[:])
             nc.vector.tensor_copy(window[:, t * P : (t + 1) * P], flipped[:])
+
+        last_blocks = tokens[:, S // P - BANK // P :, :].rearrange("p t k -> p (t k)")
+        for repeat in range(2):
+            unread = banks.tile([P, BANK], F32, name="unread", tag="bank")
+            nc.tensor.matmul(unread[:], tokens[:, S // P - 1, :], last_blocks, start=True, stop=True)
 
         for piece in range(N // PIECE):
             picked = window[:].indirect(offsets[:, piece * (PIECE // 16) : (piece + 1) * (PIECE // 16)])

@@ -36,15 +36,15 @@ def tile_gather_matmul_kernel(tc, table, w, b, offs, out):
         bias = held.tile([P, M // P], F32, name="bias")
         nc.sync.dma_start(bias[:], b.rearrange("(a p) o -> p (a o)", p=P))
 
+        zeros = held.tile([P, P], BF16, name="zeros")
+        nc.gpsimd.memset(zeros[:], 0.0)
         identity = held.tile([P, P], BF16, name="identity")
         make_identity(nc, identity[:])
 
-        zeros = held.tile([P, P], BF16, name="zeros")
-        nc.vector.memset(zeros[:], 0.0)
-        for columns in (BANK, BANK, BANK // 2):
-            unread = banks.tile([P, columns // P, P], F32, name="unread", tag="bank")
+        for repeat in range(3):
+            unread = banks.tile([P, BANK // P, P], F32, name="unread", tag="bank")
             nc.tensor.matmul(
-                unread[:], zeros[:], zeros[:].unsqueeze(1).to_broadcast([P, columns // P, P]), start=True, stop=True
+                unread[:], zeros[:], zeros[:].unsqueeze(1).to_broadcast([P, BANK // P, P]), start=True, stop=True
             )
 
         window = held.tile([K, S], BF16, name="window")

@@ -54,9 +54,8 @@ def tile_gather_matmul_kernel(tc, table, w, b, offs, out):
             nc.vector.tensor_copy(window[:, t * P : (t + 1) * P], flipped[:])
 
         last_blocks = tokens[:, S // P - BANK // P :, :].rearrange("p t k -> p (t k)")
-        for repeat in range(2):
-            unread = banks.tile([P, BANK], F32, name="unread", tag="bank")
-            nc.tensor.matmul(unread[:], tokens[:, S // P - 1, :], last_blocks, start=True, stop=True)
+        unread = banks.tile([P, BANK], F32, name="unread", tag="bank")
+        nc.tensor.matmul(unread[:], tokens[:, S // P - 1, :], last_blocks, start=True, stop=True)
 
         for piece in range(N // PIECE):
             picked = window[:].indirect(offsets[:, piece * (PIECE // 16) : (piece + 1) * (PIECE // 16)])

import concourse.mybir as mybir
from concourse.masks import make_identity

P = 128
S, K, M, N = 1024, 128, 256, 1024
BANK = 512
PIECE = 256
FLOPS = 2 * K * M * N

BF16, F32, U16 = mybir.dt.bfloat16, mybir.dt.float32, mybir.dt.uint16
ADD, MAX = mybir.AluOpType.add, mybir.AluOpType.max


def tile_gather_matmul_kernel(tc, table, w, b, offs, out):
    nc = tc.nc
    with (
        tc.tile_pool(name="held", bufs=1) as held,
        tc.tile_pool(name="results", bufs=(N // PIECE) * (M // P)) as results,
        tc.psum_pool(name="banks", bufs=8) as banks,
    ):
        tokens = held.tile([P, S // P, K], BF16, name="tokens")
        by_block = table.rearrange("(t p) k -> p t k", p=P)
        first_block = 0
        for blocks in (2, 2, 2, 1, 1):
            nc.sync.dma_start(
                tokens[:, first_block : first_block + blocks, :], by_block[:, first_block : first_block + blocks, :]
            )
            first_block += blocks

        offsets = held.tile([P, N // 16], U16, name="offsets")
        nc.sync.dma_start(offsets[:], offs)

        weights = held.tile([K, M], BF16, name="weights")
        nc.sync.dma_start(weights[:], w)

        bias = held.tile([P, M // P], F32, name="bias")
        nc.sync.dma_start(bias[:], b.rearrange("(a p) o -> p (a o)", p=P))

        zeros = held.tile([P, P], BF16, name="zeros")
        nc.gpsimd.memset(zeros[:], 0.0)
        identity = held.tile([P, P], BF16, name="identity")
        make_identity(nc, identity[:])

        for repeat in range(3):
            unread = banks.tile([P, BANK // P, P], F32, name="unread", tag="bank")
            nc.tensor.matmul(
                unread[:], zeros[:], zeros[:].unsqueeze(1).to_broadcast([P, BANK // P, P]), start=True, stop=True
            )

        window = held.tile([K, S], BF16, name="window")
        for t in range(S // P):
            flipped = banks.tile([K, P], BF16, name="flipped", tag="bank")
            nc.tensor.transpose(flipped[:], tokens[:, t, :], identity[:])
            nc.vector.tensor_copy(window[:, t * P : (t + 1) * P], flipped[:])

        last_blocks = tokens[:, S // P - BANK // P :, :].rearrange("p t k -> p (t k)")
        unread = banks.tile([P, BANK], F32, name="unread", tag="bank")
        nc.tensor.matmul(unread[:], tokens[:, S // P - 1, :], last_blocks, start=True, stop=True)

        for piece in range(N // PIECE):
            picked = window[:].indirect(offsets[:, piece * (PIECE // 16) : (piece + 1) * (PIECE // 16)])
            for a in range(M // P):
                bank = banks.tile([P, PIECE], F32, name="bank")
                nc.tensor.matmul(bank[:], weights[:, a * P : (a + 1) * P], picked, start=True, stop=True)
                result = results.tile([P, PIECE], F32, name="result")
                nc.vector.tensor_scalar(result[:], bank[:], bias[:, a : a + 1], 0.0, ADD, MAX)
                nc.sync.dma_start(out[a * P : (a + 1) * P, piece * PIECE : (piece + 1) * PIECE], result[:])
